import numpy as np
import ml_dtypes


def mxq(x, axis, fmt="e4m3"):
    dtype, down = {"e4m3": (ml_dtypes.float8_e4m3fn, 7), "e5m2": (ml_dtypes.float8_e5m2, 14)}[fmt]
    v = np.moveaxis(np.asarray(x, np.float32).astype(ml_dtypes.bfloat16).astype(np.float64), axis, -1)
    blocks = v.reshape(v.shape[:-1] + (-1, 32))
    amax = np.abs(blocks).max(-1, keepdims=True)
    byte = np.maximum(np.where(amax > 0, np.frexp(amax)[1] - 1 + 127, 0) - down, 1)
    scale = np.exp2(byte - 127.0)
    codes = (blocks / scale).astype(np.float32).astype(dtype).astype(np.float64)
    return np.moveaxis((codes * scale).reshape(v.shape), -1, axis)


WIDE = False


def mx_kscale(k):
    if not WIDE:
        return np.ones(k)
    levels = np.array([10, -10, 5, -5, 0])
    if k % 512:
        return np.exp2(np.random.permutation(np.resize(levels, k // 32))).repeat(32)
    a = np.empty((k // 512, 16))
    for p in range(k // 512):
        a[p, :8] = np.random.permutation(np.resize(levels, 8))
        for g in range(8):
            far = levels[np.abs(levels - a[p, g]) >= 10]
            a[p, g + 8] = far[np.random.randint(len(far))]
    return np.exp2(a.ravel()).repeat(32)


def f64(x):
    return np.asarray(x).astype(np.float64)


def striped(idx):
    return np.tile(idx.reshape(-1, 16).T, (8, 1)).astype(np.uint16)


def unstriped(offs):
    return offs[:16].T.reshape(-1).astype(np.int64)


def striped8(idx):
    return np.concatenate([x.reshape(-1, 16).T for x in idx]).astype(np.uint16)


def runs(offs, k):
    lists = np.stack([offs[16 * r : 16 * r + 16].T.reshape(-1) for r in range(8)]).astype(np.int64)
    return lists[np.arange(k) % 512 // 64]


def pack_weight(w):
    k, n = w.shape
    w = f64(np.asarray(w, np.float32).astype(ml_dtypes.bfloat16)).reshape(k // 32, 32, n)
    amax = np.abs(w).max(1)
    byte = np.clip(np.where(amax > 0, np.frexp(amax)[1] - 1 + 127 - 7, 1), 1, 254)
    scaled = (w * np.exp2(127.0 - byte)[:, None, :]).reshape(k, n).astype(np.float32)
    words = np.ascontiguousarray(scaled.reshape(k // 512, 128, 4, n).transpose(0, 1, 3, 2)).astype(ml_dtypes.float8_e4m3fn).view(np.uint8)
    return words, np.ascontiguousarray(byte.astype(np.uint8).reshape(k // 512, 16, n))


def unpack_weight(words, scales):
    g, p, n, _ = words.shape
    vals = np.ascontiguousarray(words).view(ml_dtypes.float8_e4m3fn).astype(np.float64) * np.repeat(np.exp2(scales.astype(np.float64) - 127.0), 8, axis=1)[..., None]
    return vals.transpose(0, 1, 3, 2).reshape(g * 512, n)


E2M1 = np.array([0.0, 0.5, 1.0, 1.5, 2.0, 3.0, 4.0, 6.0, -0.0, -0.5, -1.0, -1.5, -2.0, -3.0, -4.0, -6.0])


def pack_fp4(w):
    k, n = w.shape
    w = f64(np.asarray(w, np.float32).astype(ml_dtypes.bfloat16)).reshape(k // 32, 32, n)
    amax = np.abs(w).max(1)
    mant, ex = np.frexp(amax / 6.0)
    byte = np.clip(np.where(amax > 0, np.where(mant > 0.5, ex, ex - 1) + 127, 1), 1, 254)
    scaled = (w * np.exp2(127.0 - byte)[:, None, :]).reshape(k, n).astype(np.float32)
    c = np.ascontiguousarray(scaled.reshape(k // 512, 128, 4, n).transpose(0, 1, 3, 2)).astype(ml_dtypes.float4_e2m1fn).view(np.uint8) & 0xF
    words = (c[..., 0::2] | (c[..., 1::2] << 4)).reshape(k // 512, 128, 2 * n)
    return np.ascontiguousarray(words), np.ascontiguousarray(byte.astype(np.uint8).reshape(k // 512, 16, n))


def unpack_fp4(words, scales):
    g, _, n = scales.shape
    words = np.ascontiguousarray(words).reshape(g, 128, n, 2)
    nib = np.empty((g, 128, n, 4), np.uint8)
    nib[..., 0::2] = words & 0xF
    nib[..., 1::2] = words >> 4
    vals = E2M1[nib] * np.repeat(np.exp2(scales.astype(np.float64) - 127.0), 8, axis=1)[..., None]
    return vals.transpose(0, 1, 3, 2).reshape(g * 512, n)


def planes(y):
    n, m = y.shape
    v = y.astype(np.float32).astype(ml_dtypes.bfloat16).astype(np.float64).reshape(n // 32, 32, m)
    top = np.abs(v).max(1)
    byte = np.clip(np.where(top > 0, np.frexp(top)[1] - 1 + 127 - 7, 1), 1, 254)
    codes = (v * np.exp2(127.0 - byte)[:, None, :]).reshape(n, m).astype(np.float32).astype(ml_dtypes.float8_e4m3fn).view(np.uint8)
    words = codes.reshape(n // 512, 128, 4, m).transpose(0, 1, 3, 2)
    return np.ascontiguousarray(words), np.ascontiguousarray(byte.astype(np.uint8).reshape(n // 512, 16, m))


K, T, S, N, H = 512, 2048, 512, 512, 512


def setup_inputs():
    n = np.random.standard_normal
    s = mx_kscale(K)[:, None]
    u = mx_kscale(H)
    packed_xT = pack_weight(n((K, T)) * s)
    packed_w1 = pack_fp4(n((K, H)) / np.sqrt(K) / s)
    packed_w2 = pack_fp4(n((K, H)) / np.sqrt(K) / s)
    packed_w3 = pack_fp4(n((H, N)) / np.sqrt(H) / u[:, None])
    return {
        "x_words": packed_xT[0],
        "x_scales": packed_xT[1],
        "w1_words": packed_w1[0],
        "w1_scales": packed_w1[1],
        "w2_words": packed_w2[0],
        "w2_scales": packed_w2[1],
        "gn": (np.random.uniform(0.5, 1.5, (H, 1)) * u[:, None]).astype(np.float32),
        "w3_words": packed_w3[0],
        "w3_scales": packed_w3[1],
        "offs": striped(np.random.permutation(T)[:S]),
        "hz": striped8(np.random.randint(0, T, (8, S))),
        "n1": striped(np.random.permutation(S)),
        "n2": striped(np.random.permutation(S)),
        "n3": striped(np.random.permutation(S)),
        "n4": striped8(np.stack([np.random.permutation(S) for _ in range(8)])),
        "n5": striped8(np.stack([np.random.permutation(S) for _ in range(8)])),
    }


def reference(x_words, x_scales, w1_words, w1_scales, w2_words, w2_scales, gn, w3_words, w3_scales, offs, hz, n1, n2, n3, n4, n5):
    xq = unpack_weight(x_words, x_scales)[:, unstriped(offs)]
    y = unpack_fp4(w1_words, w1_scales).T @ xq
    x_hz = unpack_weight(x_words, x_scales)[np.arange(K)[:, None], runs(hz, K)]
    d = unpack_fp4(w2_words, w2_scales).T @ x_hz
    z = f64(gn) * (np.maximum(np.minimum(y - (0.5 * y[:, unstriped(n1)]), d[:, unstriped(n2)]), d[:, unstriped(n3)]))
    h = unpack_fp4(w3_words, w3_scales).T @ mxq(z, 0, "e4m3")
    pa = h[np.arange(N)[:, None], runs(n4, N)]
    pb = h[np.arange(N)[:, None], runs(n5, N)]
    out_0 = np.maximum(np.minimum(h, pa), np.minimum(np.maximum(h, pa), pb))
    return (out_0,) + planes(out_0)

@@ -1,0 +1,225 @@
+from contextlib import ExitStack
+
+import concourse.mybir as mybir
+
+K, T, S, N, H = 512, 2048, 512, 512, 512
+FLOPS = 3 * 2 * 512 * 512 * 512
+
+F32 = mybir.dt.float32
+BF16 = mybir.dt.bfloat16
+I32 = mybir.dt.int32
+U32 = mybir.dt.uint32
+U16 = mybir.dt.uint16
+U8 = mybir.dt.uint8
+FP8X4 = mybir.dt.float8_e4m3fn_x4
+FP4X4 = mybir.dt.float4_e2m1fn_x4
+ALU = mybir.AluOpType
+COPY = mybir.ActivationFunctionType.Copy
+
+P = 128
+PACK = 4
+QUAD = 32
+Z_PIECES = ((0, 384), (384, 512))
+OUT_PIECES = ((0, 256), (256, 512))
+
+
+def tile_picked_twhclampbmed_none_po_kernel(
+    tc, x_words, x_scales, w1_words, w1_scales, w2_words, w2_scales, gn, w3_words, w3_scales,
+    offs, hz, n1, n2, n3, n4, n5, out_0, out_1, out_2,
+):
+    nc = tc.nc
+    with ExitStack() as ctx:
+        keep = ctx.enter_context(tc.tile_pool(name="keep", bufs=1))
+        psum = ctx.enter_context(tc.psum_pool(name="psum", bufs=1))
+
+        def sb(name, shape, dtype, tag=None):
+            return keep.tile(shape, dtype, name=name, tag=tag or name, align_bytes=64)
+
+        def load_list(name, src):
+            tile = keep.tile([P, S // 16], U16, name=name)
+            nc.sync.dma_start(tile[:], src)
+            return tile
+
+        def load_scale_rows(queue, dst, src):
+            for q in range(PACK):
+                rows = src[0, PACK * q : PACK * (q + 1), :].bitcast(I32)
+                queue.dma_start(dst[QUAD * q : QUAD * (q + 1), :].bitcast(I32), rows.partition_broadcast(QUAD // PACK))
+
+        xs_win = sb("xs_win", [P, T], U8)
+        ws_raw = [sb("ws_raw%d" % i, [P, H], U8) for i in range(2)]
+        ww_raw = [sb("ww_raw%d" % i, [P, 2 * H], U8) for i in range(2)]
+        ww = [sb("ww%d" % i, [P, 2 * H], U8) for i in range(3)]
+        ws = [sb("ws%d" % i, [P, H], U8) for i in range(3)]
+        w_words = (w1_words, w2_words, w3_words)
+        w_scales = (w1_scales, w2_scales, w3_scales)
+
+        def load_w_words(queue, i):
+            queue.dma_start(ww_raw[i][:].bitcast(I32), w_words[i][0].bitcast(I32))
+
+        def load_w_scales(queue, i):
+            load_scale_rows(queue, ws_raw[i], w_scales[i])
+
+        def deal_words(i):
+            nc.vector.tensor_copy(
+                ww[i][:].rearrange("p (t m b) -> p t m b", t=PACK, b=2),
+                ww_raw[i][:].rearrange("p (m t b) -> p t m b", t=PACK, b=2),
+            )
+
+        def deal_scales(i):
+            nc.vector.tensor_copy(
+                ws[i][:].rearrange("p (t m) -> p t m", t=PACK),
+                ws_raw[i][:].rearrange("p (m t) -> p t m", t=PACK),
+            )
+
+        hz_t = load_list("hz_t", hz)
+        load_scale_rows(nc.sync, xs_win, x_scales)
+        load_w_words(nc.sync, 0)
+        offs_t = load_list("offs_t", offs)
+        xw_win = sb("xw_win", [P, T], U32)
+        nc.sync.dma_start(xw_win[:].bitcast(I32), x_words[0].rearrange("p n t -> p (n t)").bitcast(I32))
+        load_w_scales(nc.sync, 0)
+        load_w_words(nc.sync, 1)
+        load_w_scales(nc.sync, 1)
+        n1_t = load_list("n1_t", n1)
+        n2_t = load_list("n2_t", n2)
+        n3_t = load_list("n3_t", n3)
+        n4_t = load_list("n4_t", n4)
+        n5_t = load_list("n5_t", n5)
+        gn_t = keep.tile([P, PACK], F32, name="gn_t")
+        nc.gpsimd.dma_start(gn_t[:], gn.rearrange("(p t) o -> p (t o)", t=PACK))
+
+        deal_words(0)
+        xh_s_raw = sb("xh_s_raw", [P, S], U8)
+        nc.vector.tensor_copy(xh_s_raw[:], xs_win[:].indirect(hz_t[:]))
+        xh_s = sb("xh_s", [P, S], U8)
+        nc.vector.tensor_copy(xh_s[:].bitcast(I32), xh_s_raw[:].bitcast(I32))
+        for row in (2, 3):
+            nc.scalar.dma_start(xh_s[row:P:QUAD, :].bitcast(I32), xh_s_raw[16 + row:P:QUAD, :].bitcast(I32))
+        xo_s = sb("xo_s", [P, S], U8)
+        nc.vector.tensor_copy(xo_s[:], xs_win[:].indirect(offs_t[:]))
+        deal_scales(0)
+        xo_w = sb("xo_w", [P, S], U32)
+        nc.vector.tensor_copy(xo_w[:], xw_win[:].indirect(offs_t[:]))
+
+        def product(bank, i, t, codes, scales):
+            nc.tensor.matmul_mx(
+                out=bank,
+                lhsT=ww[i][:, 2 * P * t : 2 * P * (t + 1)].bitcast(FP4X4),
+                lhsT_scale=ws[i][:, P * t : P * (t + 1)],
+                rhs=codes.bitcast(FP8X4),
+                rhs_scale=scales,
+                start=True,
+                stop=True,
+            )
+
+        y_ps = [psum.tile([P, S], F32, name="y_ps%d" % t) for t in range(PACK)]
+        for t in range(PACK):
+            product(y_ps[t][:], 0, t, xo_w[:], xo_s[:])
+
+        deal_words(1)
+        deal_scales(1)
+        ww_raw.append(sb("ww_raw2", [P, 2 * H], U8, tag="ww_raw1"))
+        ws_raw.append(sb("ws_raw2", [P, H], U8, tag="ws_raw1"))
+        load_w_words(nc.sync, 2)
+        load_w_scales(nc.sync, 2)
+        xh_w = sb("xh_w", [P, S], U32)
+        nc.vector.tensor_copy(xh_w[:], xw_win[:].indirect(hz_t[:]))
+        d_ps = [psum.tile([P, S], F32, name="d_ps%d" % t, tag="dh%d" % t) for t in range(PACK)]
+        for t in range(PACK):
+            product(d_ps[t][:], 1, t, xh_w[:], xh_s[:])
+
+        y_sb = [sb("y_sb%d" % t, [P, S], F32) for t in range(PACK)]
+        d_sb = [sb("d_sb%d" % t, [P, S], F32) for t in range(PACK)]
+        g1 = sb("g1", [P, PACK, S], F32)
+        g2 = sb("g2", [P, PACK, S], F32)
+        g3 = sb("g3", [P, PACK, S], F32)
+        u = sb("u", [P, PACK, S], F32)
+        v = sb("v", [P, PACK, S], F32)
+        w = sb("w", [P, PACK, S], F32)
+        z_rows = sb("z_rows", [P, PACK, S], BF16)
+        z_grp = sb("z_grp", [P, S, PACK], BF16)
+        z_w = sb("z_w", [P, S], U32)
+        z_s = sb("z_s", [P, S], U8)
+
+        def fetch_scalar(dst, window, lst, a, b, scale=1.0):
+            nc.scalar.activation(dst, window[:].indirect(lst[:, a // 16 : b // 16]), COPY, scale=scale)
+
+        def fetch_vector(dst, window, lst, a, b):
+            nc.vector.tensor_copy(dst, window[:].indirect(lst[:, a // 16 : b // 16]))
+
+        def interleave(dst, src, a, b):
+            nc.vector.tensor_copy(
+                dst[:, a:b, :].rearrange("p (c i) t -> p c t i", i=4),
+                src[:, :, a:b].rearrange("p t (c i) -> p c t i", i=4),
+            )
+
+        h_ps = []
+        h_sb = [sb("h_sb%d" % t, [P, S], F32) for t in range(PACK)]
+        for t in range(PACK):
+            nc.vector.tensor_copy(d_sb[t][:], d_ps[t][:])
+        deal_words(2)
+        deal_scales(2)
+        for piece, (a, b) in enumerate(Z_PIECES):
+            for t in range(PACK):
+                if piece == 0:
+                    nc.scalar.copy(y_sb[t][:], y_ps[t][:])
+                fetch_scalar(g1[:, t, a:b], y_sb[t], n1_t, a, b, scale=-0.5)
+                if piece == 0 and t < 2:
+                    fetch_vector(g2[:, t, a:b], d_sb[t], n2_t, a, b)
+                else:
+                    fetch_scalar(g2[:, t, a:b], d_sb[t], n2_t, a, b)
+                fetch_scalar(g3[:, t, a:b], d_sb[t], n3_t, a, b)
+                nc.vector.tensor_tensor(u[:, t, a:b], g1[:, t, a:b], y_ps[t][:, a:b], ALU.add)
+                nc.vector.tensor_tensor(v[:, t, a:b], u[:, t, a:b], g2[:, t, a:b], ALU.min)
+                nc.vector.tensor_tensor(w[:, t, a:b], v[:, t, a:b], g3[:, t, a:b], ALU.max)
+                nc.vector.tensor_scalar(z_rows[:, t, a:b], w[:, t, a:b], gn_t[:, t : t + 1], None, ALU.mult)
+            interleave(z_grp, z_rows, a, b)
+            nc.vector.quantize_mx(
+                out=z_w[:, a:b].bitcast(FP8X4),
+                scales=z_s[:, a:b],
+                in_=z_grp[:, a:b, :].rearrange("p j t -> p (j t)"),
+            )
+            for t in range(PACK):
+                if piece == 0:
+                    h_ps.append(psum.tile([P, S], F32, name="h_ps%d" % t, tag="dh%d" % t))
+                for c in range(a, b, 256):
+                    e = min(c + 256, b)
+                    product(h_ps[t][:, c:e], 2, t, z_w[:, c:e], z_s[:, c:e])
+                nc.scalar.copy(h_sb[t][:, a:b], h_ps[t][:, a:b])
+
+        pa = sb("pa", [P, PACK, S], F32)
+        pb = sb("pb", [P, PACK, S], F32)
+        lo = sb("lo", [P, PACK, S], F32)
+        hi = sb("hi", [P, PACK, S], F32)
+        mid = sb("mid", [P, PACK, S], F32)
+        res = sb("res", [P, PACK, S], F32)
+        o_grp = sb("o_grp", [P, S, PACK], BF16)
+        o_w = sb("o_w", [P, S], U32)
+        o_s = sb("o_s", [P, S], U8)
+        out_rows = out_0.rearrange("(p t) j -> p t j", t=PACK)
+        out_words = out_1[0].rearrange("p n t -> p (n t)").bitcast(I32)
+        for piece, (a, b) in enumerate(OUT_PIECES):
+            for t in range(PACK):
+                if piece == 0 and t < 1:
+                    fetch_vector(pa[:, t, a:b], h_sb[t], n4_t, a, b)
+                else:
+                    fetch_scalar(pa[:, t, a:b], h_sb[t], n4_t, a, b)
+                fetch_scalar(pb[:, t, a:b], h_sb[t], n5_t, a, b)
+                nc.vector.tensor_tensor(hi[:, t, a:b], pa[:, t, a:b], h_ps[t][:, a:b], ALU.max)
+                nc.vector.tensor_tensor(lo[:, t, a:b], pa[:, t, a:b], h_ps[t][:, a:b], ALU.min)
+                nc.vector.tensor_tensor(mid[:, t, a:b], hi[:, t, a:b], pb[:, t, a:b], ALU.min)
+                nc.vector.tensor_tensor(res[:, t, a:b], lo[:, t, a:b], mid[:, t, a:b], ALU.max)
+                nc.sync.dma_start(out_rows[:, t, a:b], res[:, t, a:b])
+            interleave(o_grp, res, a, b)
+            nc.vector.quantize_mx(
+                out=o_w[:, a:b].bitcast(FP8X4),
+                scales=o_s[:, a:b],
+                in_=o_grp[:, a:b, :].rearrange("p j t -> p (j t)"),
+            )
+            nc.sync.dma_start(out_words[:, a:b], o_w[:, a:b].bitcast(I32))
+        for q in range(PACK):
+            queue = nc.scalar if q % 2 else nc.sync
+            queue.dma_start(
+                out_2[0, PACK * q : PACK * (q + 1), :].bitcast(I32),
+                o_s[QUAD * q : QUAD * q + PACK, :].bitcast(I32),
+            )

@@ -19,8 +19,11 @@ COPY = mybir.ActivationFunctionType.Copy
 P = 128
 PACK = 4
 QUAD = 32
-Z_PIECES = ((0, 384), (384, 512))
-OUT_PIECES = ((0, 256), (256, 512))
+ONE_LIST_WINDOW = 704
+EIGHT_LIST_WINDOW = 1024
+Z_SPLIT = 384
+OUT_SPLIT = 256
+LAST = PACK - 1
 
 
 def tile_picked_twhclampbmed_none_po_kernel(
@@ -48,7 +51,7 @@ def tile_picked_twhclampbmed_none_po_kernel(
         xs_win = sb("xs_win", [P, T], U8)
         ws_raw = [sb("ws_raw%d" % i, [P, H], U8) for i in range(2)]
         ww_raw = [sb("ww_raw%d" % i, [P, 2 * H], U8) for i in range(2)]
-        ww = [sb("ww%d" % i, [P, 2 * H], U8) for i in range(3)]
+        ww = {i: sb("ww%d" % i, [P, 2 * H], U8) for i in (0, 2)}
         ws = [sb("ws%d" % i, [P, H], U8) for i in range(3)]
         w_words = (w1_words, w2_words, w3_words)
         w_scales = (w1_scales, w2_scales, w3_scales)
@@ -60,13 +63,13 @@ def tile_picked_twhclampbmed_none_po_kernel(
             load_scale_rows(queue, ws_raw[i], w_scales[i])
 
         def deal_words(i):
-            nc.vector.tensor_copy(
+            (nc.gpsimd if i in (1, 2) else nc.vector).tensor_copy(
                 ww[i][:].rearrange("p (t m b) -> p t m b", t=PACK, b=2),
                 ww_raw[i][:].rearrange("p (m t b) -> p t m b", t=PACK, b=2),
             )
 
         def deal_scales(i):
-            nc.vector.tensor_copy(
+            (nc.gpsimd if i in (1, 2) else nc.vector).tensor_copy(
                 ws[i][:].rearrange("p (t m) -> p t m", t=PACK),
                 ws_raw[i][:].rearrange("p (m t) -> p t m", t=PACK),
             )
@@ -78,15 +81,19 @@ def tile_picked_twhclampbmed_none_po_kernel(
         xw_win = sb("xw_win", [P, T], U32)
         nc.sync.dma_start(xw_win[:].bitcast(I32), x_words[0].rearrange("p n t -> p (n t)").bitcast(I32))
         load_w_scales(nc.sync, 0)
-        load_w_words(nc.sync, 1)
+        load_w_words(nc.gpsimd, 1)
         load_w_scales(nc.sync, 1)
         n1_t = load_list("n1_t", n1)
         n2_t = load_list("n2_t", n2)
         n3_t = load_list("n3_t", n3)
         n4_t = load_list("n4_t", n4)
         n5_t = load_list("n5_t", n5)
-        gn_t = keep.tile([P, PACK], F32, name="gn_t")
-        nc.gpsimd.dma_start(gn_t[:], gn.rearrange("(p t) o -> p (t o)", t=PACK))
+
+        y_sb = [sb("y_sb%d" % t, [P, S + 16], F32) for t in range(PACK)]
+        d_sb = [sb("d_sb%d" % t, [P, ONE_LIST_WINDOW], F32) for t in range(PACK)]
+        h_sb = [sb("h_sb%d" % t, [P, EIGHT_LIST_WINDOW], F32) for t in range(PACK)]
+        for tile in y_sb + d_sb + h_sb:
+            nc.gpsimd.memset(tile[:, S:], 0.0)
 
         deal_words(0)
         xh_s_raw = sb("xh_s_raw", [P, S], U8)
@@ -98,6 +105,8 @@ def tile_picked_twhclampbmed_none_po_kernel(
         xo_s = sb("xo_s", [P, S], U8)
         nc.vector.tensor_copy(xo_s[:], xs_win[:].indirect(offs_t[:]))
         deal_scales(0)
+        gn_t = sb("gn_t", [P, PACK], F32, tag="xh_s_raw")
+        nc.sync.dma_start(gn_t[:], gn.rearrange("(p t) o -> p (t o)", t=PACK))
         xo_w = sb("xo_w", [P, S], U32)
         nc.vector.tensor_copy(xo_w[:], xw_win[:].indirect(offs_t[:]))
 
@@ -112,24 +121,26 @@ def tile_picked_twhclampbmed_none_po_kernel(
                 stop=True,
             )
 
-        y_ps = [psum.tile([P, S], F32, name="y_ps%d" % t) for t in range(PACK)]
-        for t in range(PACK):
+        def bank(name, n):
+            return psum.tile([P, S], F32, name=name, tag="bank%d" % n)
+
+        y_ps = [bank("y_ps%d" % t, t) for t in range(2)]
+        for t in range(2):
             product(y_ps[t][:], 0, t, xo_w[:], xo_s[:])
 
+        ww[1] = sb("ww1", [P, 2 * H], U8)
         deal_words(1)
         deal_scales(1)
-        ww_raw.append(sb("ww_raw2", [P, 2 * H], U8, tag="ww_raw1"))
+        ww_raw.append(sb("ww_raw2", [P, 2 * H], U8, tag="xs_win"))
         ws_raw.append(sb("ws_raw2", [P, H], U8, tag="ws_raw1"))
         load_w_words(nc.sync, 2)
         load_w_scales(nc.sync, 2)
-        xh_w = sb("xh_w", [P, S], U32)
+        xh_w = sb("xh_w", [P, S], U32, tag="ws_raw0")
         nc.vector.tensor_copy(xh_w[:], xw_win[:].indirect(hz_t[:]))
-        d_ps = [psum.tile([P, S], F32, name="d_ps%d" % t, tag="dh%d" % t) for t in range(PACK)]
+        d_ps = [bank("d_ps%d" % t, 2 + t) for t in range(PACK)]
         for t in range(PACK):
             product(d_ps[t][:], 1, t, xh_w[:], xh_s[:])
 
-        y_sb = [sb("y_sb%d" % t, [P, S], F32) for t in range(PACK)]
-        d_sb = [sb("d_sb%d" % t, [P, S], F32) for t in range(PACK)]
         g1 = sb("g1", [P, PACK, S], F32)
         g2 = sb("g2", [P, PACK, S], F32)
         g3 = sb("g3", [P, PACK, S], F32)
@@ -147,45 +158,93 @@ def tile_picked_twhclampbmed_none_po_kernel(
         def fetch_vector(dst, window, lst, a, b):
             nc.vector.tensor_copy(dst, window[:].indirect(lst[:, a // 16 : b // 16]))
 
-        def interleave(dst, src, a, b):
-            nc.vector.tensor_copy(
+        def interleave(copy, dst, src, a, b):
+            copy(
                 dst[:, a:b, :].rearrange("p (c i) t -> p c t i", i=4),
                 src[:, :, a:b].rearrange("p t (c i) -> p c t i", i=4),
             )
 
-        h_ps = []
-        h_sb = [sb("h_sb%d" % t, [P, S], F32) for t in range(PACK)]
-        for t in range(PACK):
-            nc.vector.tensor_copy(d_sb[t][:], d_ps[t][:])
+        def quantize(codes, scales, grouped, a, b):
+            nc.vector.quantize_mx(
+                out=codes[:, a:b].bitcast(FP8X4),
+                scales=scales[:, a:b],
+                in_=grouped[:, a:b, :].rearrange("p j t -> p (j t)"),
+            )
+
+
+        def shift(t, a, b):
+            nc.vector.tensor_tensor(u[:, t, a:b], g1[:, t, a:b], y_ps[t][:, a:b], ALU.add)
+
+        def cap(t, a, b):
+            nc.vector.tensor_tensor(v[:, t, a:b], u[:, t, a:b], g2[:, t, a:b], ALU.min)
+
+        def floor(t, a, b):
+            nc.vector.tensor_tensor(w[:, t, a:b], v[:, t, a:b], g3[:, t, a:b], ALU.max)
+
+        def gain(t, a, b):
+            nc.vector.tensor_scalar(z_rows[:, t, a:b], w[:, t, a:b], gn_t[:, t : t + 1], None, ALU.mult)
+
+        def spill_y(t):
+            nc.scalar.copy(y_sb[t][:, :S], y_ps[t][:])
+
+        def spill_d(t):
+            (nc.vector.tensor_copy if t == 0 else nc.scalar.copy)(d_sb[t][:, :S], d_ps[t][:])
+            if t < 2:
+                y_ps.append(bank("y_ps%d" % (t + 2), 2 + t))
+                product(y_ps[t + 2][:], 0, t + 2, xo_w[:], xo_s[:])
+
+        def fetch1(t, a, b):
+            fetch_scalar(g1[:, t, a:b], y_sb[t], n1_t, a, b, scale=-0.5)
+
+        def fetch3(t, a, b):
+            fetch_scalar(g3[:, t, a:b], d_sb[t], n3_t, a, b)
+
+        head = [S, S, Z_SPLIT, Z_SPLIT]
+        spill_y(0)
+        fetch1(0, 0, head[0])
+        spill_d(0)
         deal_words(2)
         deal_scales(2)
-        for piece, (a, b) in enumerate(Z_PIECES):
-            for t in range(PACK):
-                if piece == 0:
-                    nc.scalar.copy(y_sb[t][:], y_ps[t][:])
-                fetch_scalar(g1[:, t, a:b], y_sb[t], n1_t, a, b, scale=-0.5)
-                if piece == 0 and t < 2:
-                    fetch_vector(g2[:, t, a:b], d_sb[t], n2_t, a, b)
-                else:
-                    fetch_scalar(g2[:, t, a:b], d_sb[t], n2_t, a, b)
-                fetch_scalar(g3[:, t, a:b], d_sb[t], n3_t, a, b)
-                nc.vector.tensor_tensor(u[:, t, a:b], g1[:, t, a:b], y_ps[t][:, a:b], ALU.add)
-                nc.vector.tensor_tensor(v[:, t, a:b], u[:, t, a:b], g2[:, t, a:b], ALU.min)
-                nc.vector.tensor_tensor(w[:, t, a:b], v[:, t, a:b], g3[:, t, a:b], ALU.max)
-                nc.vector.tensor_scalar(z_rows[:, t, a:b], w[:, t, a:b], gn_t[:, t : t + 1], None, ALU.mult)
-            interleave(z_grp, z_rows, a, b)
-            nc.vector.quantize_mx(
-                out=z_w[:, a:b].bitcast(FP8X4),
-                scales=z_s[:, a:b],
-                in_=z_grp[:, a:b, :].rearrange("p j t -> p (j t)"),
-            )
-            for t in range(PACK):
-                if piece == 0:
-                    h_ps.append(psum.tile([P, S], F32, name="h_ps%d" % t, tag="dh%d" % t))
-                for c in range(a, b, 256):
-                    e = min(c + 256, b)
-                    product(h_ps[t][:, c:e], 2, t, z_w[:, c:e], z_s[:, c:e])
-                nc.scalar.copy(h_sb[t][:, a:b], h_ps[t][:, a:b])
+        for t in range(PACK):
+            if t < LAST:
+                spill_y(t + 1)
+                spill_d(t + 1)
+            fetch_vector(g2[:, t, : head[t]], d_sb[t], n2_t, 0, head[t])
+            if t > 0:
+                floor(t - 1, 0, head[t - 1])
+            shift(t, 0, head[t])
+            if t > 0:
+                gain(t - 1, 0, head[t - 1])
+            if t < LAST:
+                fetch1(t + 1, 0, head[t + 1])
+            fetch3(t, 0, head[t])
+            cap(t, 0, head[t])
+        for t in (2, 3):
+            fetch1(t, Z_SPLIT, S)
+        for t in (2, 3):
+            fetch_scalar(g2[:, t, Z_SPLIT:], d_sb[t], n2_t, Z_SPLIT, S)
+        for t in (2, 3):
+            fetch3(t, Z_SPLIT, S)
+        floor(LAST, 0, Z_SPLIT)
+        shift(2, Z_SPLIT, S)
+        gain(LAST, 0, Z_SPLIT)
+        shift(3, Z_SPLIT, S)
+        interleave(nc.vector.tensor_copy, z_grp, z_rows, 0, Z_SPLIT)
+        cap(slice(2, 4), Z_SPLIT, S)
+        quantize(z_w, z_s, z_grp, 0, Z_SPLIT)
+        floor(slice(2, 4), Z_SPLIT, S)
+        h_ps = [bank("h_ps%d" % t, n) for t, n in enumerate((6, 7, 4, 5))]
+        for t in range(PACK):
+            for a, b in ((0, 256), (256, Z_SPLIT)):
+                product(h_ps[t][:, a:b], 2, t, z_w[:, a:b], z_s[:, a:b])
+            nc.scalar.copy(h_sb[t][:, :Z_SPLIT], h_ps[t][:, :Z_SPLIT])
+        for t in (2, 3):
+            gain(t, Z_SPLIT, S)
+        interleave(nc.vector.tensor_copy, z_grp, z_rows, Z_SPLIT, S)
+        quantize(z_w, z_s, z_grp, Z_SPLIT, S)
+        for t in range(PACK):
+            product(h_ps[t][:, Z_SPLIT:], 2, t, z_w[:, Z_SPLIT:], z_s[:, Z_SPLIT:])
+            nc.vector.tensor_copy(h_sb[t][:, Z_SPLIT:S], h_ps[t][:, Z_SPLIT:])
 
         pa = sb("pa", [P, PACK, S], F32)
         pb = sb("pb", [P, PACK, S], F32)
@@ -198,25 +257,31 @@ def tile_picked_twhclampbmed_none_po_kernel(
         o_s = sb("o_s", [P, S], U8)
         out_rows = out_0.rearrange("(p t) j -> p t j", t=PACK)
         out_words = out_1[0].rearrange("p n t -> p (n t)").bitcast(I32)
-        for piece, (a, b) in enumerate(OUT_PIECES):
-            for t in range(PACK):
-                if piece == 0 and t < 1:
-                    fetch_vector(pa[:, t, a:b], h_sb[t], n4_t, a, b)
-                else:
-                    fetch_scalar(pa[:, t, a:b], h_sb[t], n4_t, a, b)
-                fetch_scalar(pb[:, t, a:b], h_sb[t], n5_t, a, b)
-                nc.vector.tensor_tensor(hi[:, t, a:b], pa[:, t, a:b], h_ps[t][:, a:b], ALU.max)
-                nc.vector.tensor_tensor(lo[:, t, a:b], pa[:, t, a:b], h_ps[t][:, a:b], ALU.min)
-                nc.vector.tensor_tensor(mid[:, t, a:b], hi[:, t, a:b], pb[:, t, a:b], ALU.min)
-                nc.vector.tensor_tensor(res[:, t, a:b], lo[:, t, a:b], mid[:, t, a:b], ALU.max)
-                nc.sync.dma_start(out_rows[:, t, a:b], res[:, t, a:b])
-            interleave(o_grp, res, a, b)
-            nc.vector.quantize_mx(
-                out=o_w[:, a:b].bitcast(FP8X4),
-                scales=o_s[:, a:b],
-                in_=o_grp[:, a:b, :].rearrange("p j t -> p (j t)"),
-            )
-            nc.sync.dma_start(out_words[:, a:b], o_w[:, a:b].bitcast(I32))
+
+        def finish(t, a, b):
+            nc.vector.tensor_tensor(res[:, t, a:b], lo[:, t, a:b], mid[:, t, a:b], ALU.max)
+            nc.sync.dma_start(out_rows[:, t, a:b], res[:, t, a:b])
+
+        steps = [(t, 0, S) for t in range(LAST)] + [(LAST, 0, OUT_SPLIT), (LAST, OUT_SPLIT, S)]
+        for n, (t, a, b) in enumerate(steps):
+            if n < 1:
+                fetch_vector(pa[:, t, a:b], h_sb[t], n4_t, a, b)
+            else:
+                fetch_scalar(pa[:, t, a:b], h_sb[t], n4_t, a, b)
+            fetch_scalar(pb[:, t, a:b], h_sb[t], n5_t, a, b)
+            nc.vector.tensor_tensor(hi[:, t, a:b], pa[:, t, a:b], h_ps[t][:, a:b], ALU.max)
+            if n > 0:
+                finish(*steps[n - 1])
+            nc.vector.tensor_tensor(lo[:, t, a:b], pa[:, t, a:b], h_ps[t][:, a:b], ALU.min)
+            nc.vector.tensor_tensor(mid[:, t, a:b], hi[:, t, a:b], pb[:, t, a:b], ALU.min)
+        (c0, c1), (e0, e1) = (0, OUT_SPLIT), (OUT_SPLIT, S)
+        interleave(nc.scalar.copy, o_grp, res, c0, c1)
+        quantize(o_w, o_s, o_grp, c0, c1)
+        nc.sync.dma_start(out_words[:, c0:c1], o_w[:, c0:c1].bitcast(I32))
+        finish(*steps[-1])
+        interleave(nc.vector.tensor_copy, o_grp, res, e0, e1)
+        quantize(o_w, o_s, o_grp, e0, e1)
+        nc.scalar.dma_start(out_words[:, e0:e1], o_w[:, e0:e1].bitcast(I32))
         for q in range(PACK):
             queue = nc.scalar if q % 2 else nc.sync
             queue.dma_start(

@@ -63,7 +63,7 @@ def tile_picked_twhclampbmed_none_po_kernel(
             load_scale_rows(queue, ws_raw[i], w_scales[i])
 
         def deal_words(i):
-            (nc.gpsimd if i in (1, 2) else nc.vector).tensor_copy(
+            (nc.gpsimd if i in (0, 1, 2) else nc.vector).tensor_copy(
                 ww[i][:].rearrange("p (t m b) -> p t m b", t=PACK, b=2),
                 ww_raw[i][:].rearrange("p (m t b) -> p t m b", t=PACK, b=2),
             )
@@ -92,7 +92,7 @@ def tile_picked_twhclampbmed_none_po_kernel(
         y_sb = [sb("y_sb%d" % t, [P, S + 16], F32) for t in range(PACK)]
         d_sb = [sb("d_sb%d" % t, [P, ONE_LIST_WINDOW], F32) for t in range(PACK)]
         h_sb = [sb("h_sb%d" % t, [P, EIGHT_LIST_WINDOW], F32) for t in range(PACK)]
-        for tile in y_sb + d_sb + h_sb:
+        for tile in y_sb + d_sb:
             nc.gpsimd.memset(tile[:, S:], 0.0)
 
         deal_words(0)
@@ -128,7 +128,7 @@ def tile_picked_twhclampbmed_none_po_kernel(
         for t in range(2):
             product(y_ps[t][:], 0, t, xo_w[:], xo_s[:])
 
-        ww[1] = sb("ww1", [P, 2 * H], U8)
+        ww[1] = sb("ww1", [P, 2 * H], U8, tag="ww_raw0")
         deal_words(1)
         deal_scales(1)
         ww_raw.append(sb("ww_raw2", [P, 2 * H], U8, tag="xs_win"))
@@ -141,10 +141,10 @@ def tile_picked_twhclampbmed_none_po_kernel(
         for t in range(PACK):
             product(d_ps[t][:], 1, t, xh_w[:], xh_s[:])
 
-        g1 = sb("g1", [P, PACK, S], F32)
+        g1 = [h_sb[t][:, S:] for t in range(PACK)]
         g2 = sb("g2", [P, PACK, S], F32)
         g3 = sb("g3", [P, PACK, S], F32)
-        u = sb("u", [P, PACK, S], F32)
+        u = sb("u", [P, PACK, S], F32, tag="ws_raw0")
         v = sb("v", [P, PACK, S], F32)
         w = sb("w", [P, PACK, S], F32)
         z_rows = sb("z_rows", [P, PACK, S], BF16)
@@ -173,7 +173,7 @@ def tile_picked_twhclampbmed_none_po_kernel(
 
 
         def shift(t, a, b):
-            nc.vector.tensor_tensor(u[:, t, a:b], g1[:, t, a:b], y_ps[t][:, a:b], ALU.add)
+            nc.vector.tensor_tensor(u[:, t, a:b], g1[t][:, a:b], y_ps[t][:, a:b], ALU.add)
 
         def cap(t, a, b):
             nc.vector.tensor_tensor(v[:, t, a:b], u[:, t, a:b], g2[:, t, a:b], ALU.min)
@@ -194,7 +194,7 @@ def tile_picked_twhclampbmed_none_po_kernel(
                 product(y_ps[t + 2][:], 0, t + 2, xo_w[:], xo_s[:])
 
         def fetch1(t, a, b):
-            fetch_scalar(g1[:, t, a:b], y_sb[t], n1_t, a, b, scale=-0.5)
+            fetch_scalar(g1[t][:, a:b], y_sb[t], n1_t, a, b, scale=-0.5)
 
         def fetch3(t, a, b):
             fetch_scalar(g3[:, t, a:b], d_sb[t], n3_t, a, b)
@@ -229,7 +229,8 @@ def tile_picked_twhclampbmed_none_po_kernel(
         shift(2, Z_SPLIT, S)
         gain(LAST, 0, Z_SPLIT)
         shift(3, Z_SPLIT, S)
-        interleave(nc.vector.tensor_copy, z_grp, z_rows, 0, Z_SPLIT)
+        interleave(nc.vector.tensor_copy, z_grp, z_rows, 0, 256)
+        interleave(nc.scalar.copy, z_grp, z_rows, 256, Z_SPLIT)
         cap(slice(2, 4), Z_SPLIT, S)
         quantize(z_w, z_s, z_grp, 0, Z_SPLIT)
         floor(slice(2, 4), Z_SPLIT, S)
@@ -276,10 +277,10 @@ def tile_picked_twhclampbmed_none_po_kernel(
             nc.vector.tensor_tensor(mid[:, t, a:b], hi[:, t, a:b], pb[:, t, a:b], ALU.min)
         (c0, c1), (e0, e1) = (0, OUT_SPLIT), (OUT_SPLIT, S)
         interleave(nc.scalar.copy, o_grp, res, c0, c1)
-        quantize(o_w, o_s, o_grp, c0, c1)
-        nc.sync.dma_start(out_words[:, c0:c1], o_w[:, c0:c1].bitcast(I32))
         finish(*steps[-1])
         interleave(nc.vector.tensor_copy, o_grp, res, e0, e1)
+        quantize(o_w, o_s, o_grp, c0, c1)
+        nc.sync.dma_start(out_words[:, c0:c1], o_w[:, c0:c1].bitcast(I32))
         quantize(o_w, o_s, o_grp, e0, e1)
         nc.scalar.dma_start(out_words[:, e0:e1], o_w[:, e0:e1].bitcast(I32))
         for q in range(PACK):

@@ -2,7 +2,7 @@ from contextlib import ExitStack
 
 import concourse.mybir as mybir
 
-K, T, S, N, H = 512, 2048, 512, 512, 512
+T, S, H = 2048, 512, 512
 FLOPS = 3 * 2 * 512 * 512 * 512
 
 F32 = mybir.dt.float32
@@ -19,11 +19,16 @@ COPY = mybir.ActivationFunctionType.Copy
 P = 128
 PACK = 4
 QUAD = 32
-ONE_LIST_WINDOW = 704
-EIGHT_LIST_WINDOW = 1024
-Z_SPLIT = 384
-OUT_SPLIT = 256
+GROUP = 16
 LAST = PACK - 1
+W1, W2, W3 = 0, 1, 2
+
+Y_WINDOW = S + 16
+D_WINDOW = 704
+H_WINDOW = 2 * S
+HALF = S // 2
+Z_SPLIT = 384
+SPLIT_TILES = (2, 3)
 
 
 def tile_picked_twhclampbmed_none_po_kernel(
@@ -38,81 +43,79 @@ def tile_picked_twhclampbmed_none_po_kernel(
         def sb(name, shape, dtype, tag=None):
             return keep.tile(shape, dtype, name=name, tag=tag or name, align_bytes=64)
 
+        def bank(name, n):
+            return psum.tile([P, S], F32, name=name, tag="bank%d" % n)
+
         def load_list(name, src):
-            tile = keep.tile([P, S // 16], U16, name=name)
+            tile = keep.tile([P, S // GROUP], U16, name=name)
             nc.sync.dma_start(tile[:], src)
             return tile
 
-        def load_scale_rows(queue, dst, src):
+        def load_scale_rows(dst, src):
             for q in range(PACK):
                 rows = src[0, PACK * q : PACK * (q + 1), :].bitcast(I32)
-                queue.dma_start(dst[QUAD * q : QUAD * (q + 1), :].bitcast(I32), rows.partition_broadcast(QUAD // PACK))
+                nc.sync.dma_start(dst[QUAD * q : QUAD * (q + 1), :].bitcast(I32), rows.partition_broadcast(QUAD // PACK))
 
         xs_win = sb("xs_win", [P, T], U8)
-        ws_raw = [sb("ws_raw%d" % i, [P, H], U8) for i in range(2)]
-        ww_raw = [sb("ww_raw%d" % i, [P, 2 * H], U8) for i in range(2)]
-        ww = {i: sb("ww%d" % i, [P, 2 * H], U8) for i in (0, 2)}
-        ws = [sb("ws%d" % i, [P, H], U8) for i in range(3)]
-        w_words = (w1_words, w2_words, w3_words)
-        w_scales = (w1_scales, w2_scales, w3_scales)
+        ws_raw = [sb("ws_raw%d" % i, [P, H], U8) for i in (W1, W2)]
+        ww_raw = [sb("ww_raw%d" % i, [P, 2 * H], U8) for i in (W1, W2)]
+        ww = {i: sb("ww%d" % i, [P, 2 * H], U8) for i in (W1, W3)}
+        ws = [sb("ws%d" % i, [P, H], U8) for i in (W1, W2, W3)]
 
-        def load_w_words(queue, i):
-            queue.dma_start(ww_raw[i][:].bitcast(I32), w_words[i][0].bitcast(I32))
-
-        def load_w_scales(queue, i):
-            load_scale_rows(queue, ws_raw[i], w_scales[i])
+        def load_w_words(queue, i, src):
+            queue.dma_start(ww_raw[i][:].bitcast(I32), src[0].bitcast(I32))
 
         def deal_words(i):
-            (nc.gpsimd if i in (0, 1, 2) else nc.vector).tensor_copy(
+            nc.gpsimd.tensor_copy(
                 ww[i][:].rearrange("p (t m b) -> p t m b", t=PACK, b=2),
                 ww_raw[i][:].rearrange("p (m t b) -> p t m b", t=PACK, b=2),
             )
 
-        def deal_scales(i):
-            (nc.gpsimd if i in (1, 2) else nc.vector).tensor_copy(
+        def deal_scales(engine, i):
+            engine.tensor_copy(
                 ws[i][:].rearrange("p (t m) -> p t m", t=PACK),
                 ws_raw[i][:].rearrange("p (m t) -> p t m", t=PACK),
             )
 
         hz_t = load_list("hz_t", hz)
-        load_scale_rows(nc.sync, xs_win, x_scales)
-        load_w_words(nc.sync, 0)
+        load_scale_rows(xs_win, x_scales)
+        load_w_words(nc.sync, W1, w1_words)
         offs_t = load_list("offs_t", offs)
         xw_win = sb("xw_win", [P, T], U32)
         nc.sync.dma_start(xw_win[:].bitcast(I32), x_words[0].rearrange("p n t -> p (n t)").bitcast(I32))
-        load_w_scales(nc.sync, 0)
-        load_w_words(nc.gpsimd, 1)
-        load_w_scales(nc.sync, 1)
+        load_scale_rows(ws_raw[W1], w1_scales)
+        load_w_words(nc.gpsimd, W2, w2_words)
+        load_scale_rows(ws_raw[W2], w2_scales)
         n1_t = load_list("n1_t", n1)
         n2_t = load_list("n2_t", n2)
         n3_t = load_list("n3_t", n3)
         n4_t = load_list("n4_t", n4)
         n5_t = load_list("n5_t", n5)
 
-        y_sb = [sb("y_sb%d" % t, [P, S + 16], F32) for t in range(PACK)]
-        d_sb = [sb("d_sb%d" % t, [P, ONE_LIST_WINDOW], F32) for t in range(PACK)]
-        h_sb = [sb("h_sb%d" % t, [P, EIGHT_LIST_WINDOW], F32) for t in range(PACK)]
+        y_sb = [sb("y_sb%d" % t, [P, Y_WINDOW], F32) for t in range(PACK)]
+        d_sb = [sb("d_sb%d" % t, [P, D_WINDOW], F32) for t in range(PACK)]
+        h_sb = [sb("h_sb%d" % t, [P, H_WINDOW], F32) for t in range(PACK)]
         for tile in y_sb + d_sb:
             nc.gpsimd.memset(tile[:, S:], 0.0)
 
-        deal_words(0)
+        deal_words(W1)
         xh_s_raw = sb("xh_s_raw", [P, S], U8)
         nc.vector.tensor_copy(xh_s_raw[:], xs_win[:].indirect(hz_t[:]))
         xh_s = sb("xh_s", [P, S], U8)
         nc.vector.tensor_copy(xh_s[:].bitcast(I32), xh_s_raw[:].bitcast(I32))
         for row in (2, 3):
-            nc.scalar.dma_start(xh_s[row:P:QUAD, :].bitcast(I32), xh_s_raw[16 + row:P:QUAD, :].bitcast(I32))
+            nc.scalar.dma_start(xh_s[row:P:QUAD, :].bitcast(I32), xh_s_raw[GROUP + row : P : QUAD, :].bitcast(I32))
         xo_s = sb("xo_s", [P, S], U8)
         nc.vector.tensor_copy(xo_s[:], xs_win[:].indirect(offs_t[:]))
-        deal_scales(0)
+        deal_scales(nc.vector, W1)
         gn_t = sb("gn_t", [P, PACK], F32, tag="xh_s_raw")
         nc.sync.dma_start(gn_t[:], gn.rearrange("(p t) o -> p (t o)", t=PACK))
         xo_w = sb("xo_w", [P, S], U32)
         nc.vector.tensor_copy(xo_w[:], xw_win[:].indirect(offs_t[:]))
 
-        def product(bank, i, t, codes, scales):
+        def product(dst, i, t, codes, scales):
             nc.tensor.matmul_mx(
-                out=bank,
+                out=dst,
                 lhsT=ww[i][:, 2 * P * t : 2 * P * (t + 1)].bitcast(FP4X4),
                 lhsT_scale=ws[i][:, P * t : P * (t + 1)],
                 rhs=codes.bitcast(FP8X4),
@@ -121,42 +124,39 @@ def tile_picked_twhclampbmed_none_po_kernel(
                 stop=True,
             )
 
-        def bank(name, n):
-            return psum.tile([P, S], F32, name=name, tag="bank%d" % n)
+        y_ps = [bank("y_ps%d" % t, t) for t in (0, 1)]
+        for t in (0, 1):
+            product(y_ps[t][:], W1, t, xo_w[:], xo_s[:])
 
-        y_ps = [bank("y_ps%d" % t, t) for t in range(2)]
-        for t in range(2):
-            product(y_ps[t][:], 0, t, xo_w[:], xo_s[:])
-
-        ww[1] = sb("ww1", [P, 2 * H], U8, tag="ww_raw0")
-        deal_words(1)
-        deal_scales(1)
+        ww[W2] = sb("ww1", [P, 2 * H], U8, tag="ww_raw0")
+        deal_words(W2)
+        deal_scales(nc.gpsimd, W2)
         ww_raw.append(sb("ww_raw2", [P, 2 * H], U8, tag="xs_win"))
         ws_raw.append(sb("ws_raw2", [P, H], U8, tag="ws_raw1"))
-        load_w_words(nc.sync, 2)
-        load_w_scales(nc.sync, 2)
+        load_w_words(nc.sync, W3, w3_words)
+        load_scale_rows(ws_raw[W3], w3_scales)
         xh_w = sb("xh_w", [P, S], U32, tag="ws_raw0")
         nc.vector.tensor_copy(xh_w[:], xw_win[:].indirect(hz_t[:]))
         d_ps = [bank("d_ps%d" % t, 2 + t) for t in range(PACK)]
         for t in range(PACK):
-            product(d_ps[t][:], 1, t, xh_w[:], xh_s[:])
+            product(d_ps[t][:], W2, t, xh_w[:], xh_s[:])
 
-        g1 = [h_sb[t][:, S:] for t in range(PACK)]
-        g2 = sb("g2", [P, PACK, S], F32)
-        g3 = sb("g3", [P, PACK, S], F32)
-        u = sb("u", [P, PACK, S], F32, tag="ws_raw0")
-        v = sb("v", [P, PACK, S], F32)
-        w = sb("w", [P, PACK, S], F32)
+        half_y = [h_sb[t][:, S:] for t in range(PACK)]
+        d_n2 = sb("d_n2", [P, PACK, S], F32)
+        d_n3 = sb("d_n3", [P, PACK, S], F32)
+        shifted = sb("shifted", [P, PACK, S], F32)
+        capped = sb("capped", [P, PACK, S], F32)
+        floored = sb("floored", [P, PACK, S], F32)
         z_rows = sb("z_rows", [P, PACK, S], BF16)
         z_grp = sb("z_grp", [P, S, PACK], BF16)
         z_w = sb("z_w", [P, S], U32)
         z_s = sb("z_s", [P, S], U8)
 
         def fetch_scalar(dst, window, lst, a, b, scale=1.0):
-            nc.scalar.activation(dst, window[:].indirect(lst[:, a // 16 : b // 16]), COPY, scale=scale)
+            nc.scalar.activation(dst, window[:].indirect(lst[:, a // GROUP : b // GROUP]), COPY, scale=scale)
 
         def fetch_vector(dst, window, lst, a, b):
-            nc.vector.tensor_copy(dst, window[:].indirect(lst[:, a // 16 : b // 16]))
+            nc.vector.tensor_copy(dst, window[:].indirect(lst[:, a // GROUP : b // GROUP]))
 
         def interleave(copy, dst, src, a, b):
             copy(
@@ -171,81 +171,86 @@ def tile_picked_twhclampbmed_none_po_kernel(
                 in_=grouped[:, a:b, :].rearrange("p j t -> p (j t)"),
             )
 
-
         def shift(t, a, b):
-            nc.vector.tensor_tensor(u[:, t, a:b], g1[t][:, a:b], y_ps[t][:, a:b], ALU.add)
+            nc.vector.tensor_tensor(shifted[:, t, a:b], half_y[t][:, a:b], y_ps[t][:, a:b], ALU.add)
 
         def cap(t, a, b):
-            nc.vector.tensor_tensor(v[:, t, a:b], u[:, t, a:b], g2[:, t, a:b], ALU.min)
+            nc.vector.tensor_tensor(capped[:, t, a:b], shifted[:, t, a:b], d_n2[:, t, a:b], ALU.min)
 
         def floor(t, a, b):
-            nc.vector.tensor_tensor(w[:, t, a:b], v[:, t, a:b], g3[:, t, a:b], ALU.max)
+            nc.vector.tensor_tensor(floored[:, t, a:b], capped[:, t, a:b], d_n3[:, t, a:b], ALU.max)
 
         def gain(t, a, b):
-            nc.vector.tensor_scalar(z_rows[:, t, a:b], w[:, t, a:b], gn_t[:, t : t + 1], None, ALU.mult)
+            nc.vector.tensor_scalar(z_rows[:, t, a:b], floored[:, t, a:b], gn_t[:, t : t + 1], None, ALU.mult)
 
         def spill_y(t):
             nc.scalar.copy(y_sb[t][:, :S], y_ps[t][:])
 
         def spill_d(t):
             (nc.vector.tensor_copy if t == 0 else nc.scalar.copy)(d_sb[t][:, :S], d_ps[t][:])
-            if t < 2:
+            if t in (0, 1):
                 y_ps.append(bank("y_ps%d" % (t + 2), 2 + t))
-                product(y_ps[t + 2][:], 0, t + 2, xo_w[:], xo_s[:])
+                product(y_ps[t + 2][:], W1, t + 2, xo_w[:], xo_s[:])
 
-        def fetch1(t, a, b):
-            fetch_scalar(g1[t][:, a:b], y_sb[t], n1_t, a, b, scale=-0.5)
+        def fetch_n1(t, a, b):
+            fetch_scalar(half_y[t][:, a:b], y_sb[t], n1_t, a, b, scale=-0.5)
 
-        def fetch3(t, a, b):
-            fetch_scalar(g3[:, t, a:b], d_sb[t], n3_t, a, b)
+        def fetch_n3(t, a, b):
+            fetch_scalar(d_n3[:, t, a:b], d_sb[t], n3_t, a, b)
 
-        head = [S, S, Z_SPLIT, Z_SPLIT]
+        first_end = [Z_SPLIT if t in SPLIT_TILES else S for t in range(PACK)]
         spill_y(0)
-        fetch1(0, 0, head[0])
+        fetch_n1(0, 0, first_end[0])
         spill_d(0)
-        deal_words(2)
-        deal_scales(2)
+        deal_words(W3)
+        deal_scales(nc.gpsimd, W3)
         for t in range(PACK):
             if t < LAST:
                 spill_y(t + 1)
                 spill_d(t + 1)
-            fetch_vector(g2[:, t, : head[t]], d_sb[t], n2_t, 0, head[t])
+            fetch_vector(d_n2[:, t, : first_end[t]], d_sb[t], n2_t, 0, first_end[t])
             if t > 0:
-                floor(t - 1, 0, head[t - 1])
-            shift(t, 0, head[t])
+                floor(t - 1, 0, first_end[t - 1])
+            shift(t, 0, first_end[t])
             if t > 0:
-                gain(t - 1, 0, head[t - 1])
+                gain(t - 1, 0, first_end[t - 1])
             if t < LAST:
-                fetch1(t + 1, 0, head[t + 1])
-            fetch3(t, 0, head[t])
-            cap(t, 0, head[t])
-        for t in (2, 3):
-            fetch1(t, Z_SPLIT, S)
-        for t in (2, 3):
-            fetch_scalar(g2[:, t, Z_SPLIT:], d_sb[t], n2_t, Z_SPLIT, S)
-        for t in (2, 3):
-            fetch3(t, Z_SPLIT, S)
+                fetch_n1(t + 1, 0, first_end[t + 1])
+            fetch_n3(t, 0, first_end[t])
+            cap(t, 0, first_end[t])
+
+        both = slice(SPLIT_TILES[0], SPLIT_TILES[-1] + 1)
+        for t in SPLIT_TILES:
+            fetch_n1(t, Z_SPLIT, S)
+        for t in SPLIT_TILES:
+            fetch_scalar(d_n2[:, t, Z_SPLIT:], d_sb[t], n2_t, Z_SPLIT, S)
+        for t in SPLIT_TILES:
+            fetch_n3(t, Z_SPLIT, S)
         floor(LAST, 0, Z_SPLIT)
-        shift(2, Z_SPLIT, S)
+        shift(SPLIT_TILES[0], Z_SPLIT, S)
         gain(LAST, 0, Z_SPLIT)
-        shift(3, Z_SPLIT, S)
-        interleave(nc.vector.tensor_copy, z_grp, z_rows, 0, 256)
-        interleave(nc.scalar.copy, z_grp, z_rows, 256, Z_SPLIT)
-        cap(slice(2, 4), Z_SPLIT, S)
-        quantize(z_w, z_s, z_grp, 0, Z_SPLIT)
-        floor(slice(2, 4), Z_SPLIT, S)
+        shift(SPLIT_TILES[1], Z_SPLIT, S)
+        interleave(nc.vector.tensor_copy, z_grp, z_rows, 0, HALF)
+        interleave(nc.scalar.copy, z_grp, z_rows, HALF, Z_SPLIT)
+        cap(both, Z_SPLIT, S)
+        quantize(z_w, z_s, z_grp, 0, HALF)
+        floor(both, Z_SPLIT, S)
+
         h_ps = [bank("h_ps%d" % t, n) for t, n in enumerate((6, 7, 4, 5))]
         for t in range(PACK):
-            for a, b in ((0, 256), (256, Z_SPLIT)):
-                product(h_ps[t][:, a:b], 2, t, z_w[:, a:b], z_s[:, a:b])
-            nc.scalar.copy(h_sb[t][:, :Z_SPLIT], h_ps[t][:, :Z_SPLIT])
-        for t in (2, 3):
+            product(h_ps[t][:, :HALF], W3, t, z_w[:, :HALF], z_s[:, :HALF])
+            nc.scalar.copy(h_sb[t][:, :HALF], h_ps[t][:, :HALF])
+        for t in SPLIT_TILES:
             gain(t, Z_SPLIT, S)
         interleave(nc.vector.tensor_copy, z_grp, z_rows, Z_SPLIT, S)
-        quantize(z_w, z_s, z_grp, Z_SPLIT, S)
+        quantize(z_w, z_s, z_grp, HALF, S)
         for t in range(PACK):
-            product(h_ps[t][:, Z_SPLIT:], 2, t, z_w[:, Z_SPLIT:], z_s[:, Z_SPLIT:])
-            nc.vector.tensor_copy(h_sb[t][:, Z_SPLIT:S], h_ps[t][:, Z_SPLIT:])
+            product(h_ps[t][:, HALF:], W3, t, z_w[:, HALF:], z_s[:, HALF:])
+
+        def spill_upper_h(t):
+            (nc.vector.tensor_copy if t in (0, 1) else nc.scalar.copy)(h_sb[t][:, HALF:S], h_ps[t][:, HALF:])
+
+        spill_upper_h(0)
 
         pa = sb("pa", [P, PACK, S], F32)
         pb = sb("pb", [P, PACK, S], F32)
@@ -263,26 +268,25 @@ def tile_picked_twhclampbmed_none_po_kernel(
             nc.vector.tensor_tensor(res[:, t, a:b], lo[:, t, a:b], mid[:, t, a:b], ALU.max)
             nc.sync.dma_start(out_rows[:, t, a:b], res[:, t, a:b])
 
-        steps = [(t, 0, S) for t in range(LAST)] + [(LAST, 0, OUT_SPLIT), (LAST, OUT_SPLIT, S)]
+        steps = [(t, 0, S) for t in range(LAST)] + [(LAST, 0, HALF), (LAST, HALF, S)]
         for n, (t, a, b) in enumerate(steps):
-            if n < 1:
-                fetch_vector(pa[:, t, a:b], h_sb[t], n4_t, a, b)
-            else:
-                fetch_scalar(pa[:, t, a:b], h_sb[t], n4_t, a, b)
+            (fetch_vector if n == 0 else fetch_scalar)(pa[:, t, a:b], h_sb[t], n4_t, a, b)
             fetch_scalar(pb[:, t, a:b], h_sb[t], n5_t, a, b)
+            if t < LAST:
+                spill_upper_h(t + 1)
             nc.vector.tensor_tensor(hi[:, t, a:b], pa[:, t, a:b], h_ps[t][:, a:b], ALU.max)
             if n > 0:
                 finish(*steps[n - 1])
             nc.vector.tensor_tensor(lo[:, t, a:b], pa[:, t, a:b], h_ps[t][:, a:b], ALU.min)
             nc.vector.tensor_tensor(mid[:, t, a:b], hi[:, t, a:b], pb[:, t, a:b], ALU.min)
-        (c0, c1), (e0, e1) = (0, OUT_SPLIT), (OUT_SPLIT, S)
-        interleave(nc.scalar.copy, o_grp, res, c0, c1)
+
+        interleave(nc.scalar.copy, o_grp, res, 0, HALF)
         finish(*steps[-1])
-        interleave(nc.vector.tensor_copy, o_grp, res, e0, e1)
-        quantize(o_w, o_s, o_grp, c0, c1)
-        nc.sync.dma_start(out_words[:, c0:c1], o_w[:, c0:c1].bitcast(I32))
-        quantize(o_w, o_s, o_grp, e0, e1)
-        nc.scalar.dma_start(out_words[:, e0:e1], o_w[:, e0:e1].bitcast(I32))
+        interleave(nc.vector.tensor_copy, o_grp, res, HALF, S)
+        quantize(o_w, o_s, o_grp, 0, HALF)
+        nc.sync.dma_start(out_words[:, :HALF], o_w[:, :HALF].bitcast(I32))
+        quantize(o_w, o_s, o_grp, HALF, S)
+        nc.scalar.dma_start(out_words[:, HALF:], o_w[:, HALF:].bitcast(I32))
         for q in range(PACK):
             queue = nc.scalar if q % 2 else nc.sync
             queue.dma_start(

from contextlib import ExitStack

import concourse.mybir as mybir

T, S, H = 2048, 512, 512
FLOPS = 3 * 2 * 512 * 512 * 512

F32 = mybir.dt.float32
BF16 = mybir.dt.bfloat16
I32 = mybir.dt.int32
U32 = mybir.dt.uint32
U16 = mybir.dt.uint16
U8 = mybir.dt.uint8
FP8X4 = mybir.dt.float8_e4m3fn_x4
FP4X4 = mybir.dt.float4_e2m1fn_x4
ALU = mybir.AluOpType
COPY = mybir.ActivationFunctionType.Copy

P = 128
PACK = 4
QUAD = 32
GROUP = 16
LAST = PACK - 1
W1, W2, W3 = 0, 1, 2

Y_WINDOW = S + 16
D_WINDOW = 704
H_WINDOW = 2 * S
HALF = S // 2
Z_SPLIT = 384
SPLIT_TILES = (2, 3)


def tile_picked_twhclampbmed_none_po_kernel(
    tc, x_words, x_scales, w1_words, w1_scales, w2_words, w2_scales, gn, w3_words, w3_scales,
    offs, hz, n1, n2, n3, n4, n5, out_0, out_1, out_2,
):
    nc = tc.nc
    with ExitStack() as ctx:
        keep = ctx.enter_context(tc.tile_pool(name="keep", bufs=1))
        psum = ctx.enter_context(tc.psum_pool(name="psum", bufs=1))

        def sb(name, shape, dtype, tag=None):
            return keep.tile(shape, dtype, name=name, tag=tag or name, align_bytes=64)

        def bank(name, n):
            return psum.tile([P, S], F32, name=name, tag="bank%d" % n)

        def load_list(name, src):
            tile = keep.tile([P, S // GROUP], U16, name=name)
            nc.sync.dma_start(tile[:], src)
            return tile

        def load_scale_rows(dst, src):
            for q in range(PACK):
                rows = src[0, PACK * q : PACK * (q + 1), :].bitcast(I32)
                nc.sync.dma_start(dst[QUAD * q : QUAD * (q + 1), :].bitcast(I32), rows.partition_broadcast(QUAD // PACK))

        xs_win = sb("xs_win", [P, T], U8)
        ws_raw = [sb("ws_raw%d" % i, [P, H], U8) for i in (W1, W2)]
        ww_raw = [sb("ww_raw%d" % i, [P, 2 * H], U8) for i in (W1, W2)]
        ww = {i: sb("ww%d" % i, [P, 2 * H], U8) for i in (W1, W3)}
        ws = [sb("ws%d" % i, [P, H], U8) for i in (W1, W2, W3)]

        def load_w_words(queue, i, src):
            queue.dma_start(ww_raw[i][:].bitcast(I32), src[0].bitcast(I32))

        def deal_words(i):
            nc.gpsimd.tensor_copy(
                ww[i][:].rearrange("p (t m b) -> p t m b", t=PACK, b=2),
                ww_raw[i][:].rearrange("p (m t b) -> p t m b", t=PACK, b=2),
            )

        def deal_scales(engine, i):
            engine.tensor_copy(
                ws[i][:].rearrange("p (t m) -> p t m", t=PACK),
                ws_raw[i][:].rearrange("p (m t) -> p t m", t=PACK),
            )

        hz_t = load_list("hz_t", hz)
        load_scale_rows(xs_win, x_scales)
        load_w_words(nc.sync, W1, w1_words)
        offs_t = load_list("offs_t", offs)
        xw_win = sb("xw_win", [P, T], U32)
        nc.sync.dma_start(xw_win[:].bitcast(I32), x_words[0].rearrange("p n t -> p (n t)").bitcast(I32))
        load_scale_rows(ws_raw[W1], w1_scales)
        load_w_words(nc.gpsimd, W2, w2_words)
        load_scale_rows(ws_raw[W2], w2_scales)
        n1_t = load_list("n1_t", n1)
        n2_t = load_list("n2_t", n2)
        n3_t = load_list("n3_t", n3)
        n4_t = load_list("n4_t", n4)
        n5_t = load_list("n5_t", n5)

        y_sb = [sb("y_sb%d" % t, [P, Y_WINDOW], F32) for t in range(PACK)]
        d_sb = [sb("d_sb%d" % t, [P, D_WINDOW], F32) for t in range(PACK)]
        h_sb = [sb("h_sb%d" % t, [P, H_WINDOW], F32) for t in range(PACK)]
        for tile in y_sb + d_sb:
            nc.gpsimd.memset(tile[:, S:], 0.0)

        deal_words(W1)
        xh_s_raw = sb("xh_s_raw", [P, S], U8)
        nc.vector.tensor_copy(xh_s_raw[:], xs_win[:].indirect(hz_t[:]))
        xh_s = sb("xh_s", [P, S], U8)
        nc.vector.tensor_copy(xh_s[:].bitcast(I32), xh_s_raw[:].bitcast(I32))
        for row in (2, 3):
            nc.scalar.dma_start(xh_s[row:P:QUAD, :].bitcast(I32), xh_s_raw[GROUP + row : P : QUAD, :].bitcast(I32))
        xo_s = sb("xo_s", [P, S], U8)
        nc.vector.tensor_copy(xo_s[:], xs_win[:].indirect(offs_t[:]))
        deal_scales(nc.vector, W1)
        gn_t = sb("gn_t", [P, PACK], F32, tag="xh_s_raw")
        nc.sync.dma_start(gn_t[:], gn.rearrange("(p t) o -> p (t o)", t=PACK))
        xo_w = sb("xo_w", [P, S], U32)
        nc.vector.tensor_copy(xo_w[:], xw_win[:].indirect(offs_t[:]))

        def product(dst, i, t, codes, scales):
            nc.tensor.matmul_mx(
                out=dst,
                lhsT=ww[i][:, 2 * P * t : 2 * P * (t + 1)].bitcast(FP4X4),
                lhsT_scale=ws[i][:, P * t : P * (t + 1)],
                rhs=codes.bitcast(FP8X4),
                rhs_scale=scales,
                start=True,
                stop=True,
            )

        y_ps = [bank("y_ps%d" % t, t) for t in (0, 1)]
        for t in (0, 1):
            product(y_ps[t][:], W1, t, xo_w[:], xo_s[:])

        ww[W2] = sb("ww1", [P, 2 * H], U8, tag="ww_raw0")
        deal_words(W2)
        deal_scales(nc.gpsimd, W2)
        ww_raw.append(sb("ww_raw2", [P, 2 * H], U8, tag="xs_win"))
        ws_raw.append(sb("ws_raw2", [P, H], U8, tag="ws_raw1"))
        load_w_words(nc.sync, W3, w3_words)
        load_scale_rows(ws_raw[W3], w3_scales)
        xh_w = sb("xh_w", [P, S], U32, tag="ws_raw0")
        nc.vector.tensor_copy(xh_w[:], xw_win[:].indirect(hz_t[:]))
        d_ps = [bank("d_ps%d" % t, 2 + t) for t in range(PACK)]
        for t in range(PACK):
            product(d_ps[t][:], W2, t, xh_w[:], xh_s[:])

        half_y = [h_sb[t][:, S:] for t in range(PACK)]
        d_n2 = sb("d_n2", [P, PACK, S], F32)
        d_n3 = sb("d_n3", [P, PACK, S], F32)
        shifted = sb("shifted", [P, PACK, S], F32)
        capped = sb("capped", [P, PACK, S], F32)
        floored = sb("floored", [P, PACK, S], F32)
        z_rows = sb("z_rows", [P, PACK, S], BF16)
        z_grp = sb("z_grp", [P, S, PACK], BF16)
        z_w = sb("z_w", [P, S], U32)
        z_s = sb("z_s", [P, S], U8)

        def fetch_scalar(dst, window, lst, a, b, scale=1.0):
            nc.scalar.activation(dst, window[:].indirect(lst[:, a // GROUP : b // GROUP]), COPY, scale=scale)

        def fetch_vector(dst, window, lst, a, b):
            nc.vector.tensor_copy(dst, window[:].indirect(lst[:, a // GROUP : b // GROUP]))

        def interleave(copy, dst, src, a, b):
            copy(
                dst[:, a:b, :].rearrange("p (c i) t -> p c t i", i=4),
                src[:, :, a:b].rearrange("p t (c i) -> p c t i", i=4),
            )

        def quantize(codes, scales, grouped, a, b):
            nc.vector.quantize_mx(
                out=codes[:, a:b].bitcast(FP8X4),
                scales=scales[:, a:b],
                in_=grouped[:, a:b, :].rearrange("p j t -> p (j t)"),
            )

        def shift(t, a, b):
            nc.vector.tensor_tensor(shifted[:, t, a:b], half_y[t][:, a:b], y_ps[t][:, a:b], ALU.add)

        def cap(t, a, b):
            nc.vector.tensor_tensor(capped[:, t, a:b], shifted[:, t, a:b], d_n2[:, t, a:b], ALU.min)

        def floor(t, a, b):
            nc.vector.tensor_tensor(floored[:, t, a:b], capped[:, t, a:b], d_n3[:, t, a:b], ALU.max)

        def gain(t, a, b):
            nc.vector.tensor_scalar(z_rows[:, t, a:b], floored[:, t, a:b], gn_t[:, t : t + 1], None, ALU.mult)

        def spill_y(t):
            nc.scalar.copy(y_sb[t][:, :S], y_ps[t][:])

        def spill_d(t):
            (nc.vector.tensor_copy if t == 0 else nc.scalar.copy)(d_sb[t][:, :S], d_ps[t][:])
            if t in (0, 1):
                y_ps.append(bank("y_ps%d" % (t + 2), 2 + t))
                product(y_ps[t + 2][:], W1, t + 2, xo_w[:], xo_s[:])

        def fetch_n1(t, a, b):
            fetch_scalar(half_y[t][:, a:b], y_sb[t], n1_t, a, b, scale=-0.5)

        def fetch_n3(t, a, b):
            fetch_scalar(d_n3[:, t, a:b], d_sb[t], n3_t, a, b)

        first_end = [Z_SPLIT if t in SPLIT_TILES else S for t in range(PACK)]
        spill_y(0)
        fetch_n1(0, 0, first_end[0])
        spill_d(0)
        deal_words(W3)
        deal_scales(nc.gpsimd, W3)
        for t in range(PACK):
            if t < LAST:
                spill_y(t + 1)
                spill_d(t + 1)
            fetch_vector(d_n2[:, t, : first_end[t]], d_sb[t], n2_t, 0, first_end[t])
            if t > 0:
                floor(t - 1, 0, first_end[t - 1])
            shift(t, 0, first_end[t])
            if t > 0:
                gain(t - 1, 0, first_end[t - 1])
            if t < LAST:
                fetch_n1(t + 1, 0, first_end[t + 1])
            fetch_n3(t, 0, first_end[t])
            cap(t, 0, first_end[t])

        both = slice(SPLIT_TILES[0], SPLIT_TILES[-1] + 1)
        for t in SPLIT_TILES:
            fetch_n1(t, Z_SPLIT, S)
        for t in SPLIT_TILES:
            fetch_scalar(d_n2[:, t, Z_SPLIT:], d_sb[t], n2_t, Z_SPLIT, S)
        for t in SPLIT_TILES:
            fetch_n3(t, Z_SPLIT, S)
        floor(LAST, 0, Z_SPLIT)
        shift(SPLIT_TILES[0], Z_SPLIT, S)
        gain(LAST, 0, Z_SPLIT)
        shift(SPLIT_TILES[1], Z_SPLIT, S)
        interleave(nc.vector.tensor_copy, z_grp, z_rows, 0, HALF)
        interleave(nc.scalar.copy, z_grp, z_rows, HALF, Z_SPLIT)
        cap(both, Z_SPLIT, S)
        quantize(z_w, z_s, z_grp, 0, HALF)
        floor(both, Z_SPLIT, S)

        h_ps = [bank("h_ps%d" % t, n) for t, n in enumerate((6, 7, 4, 5))]
        for t in range(PACK):
            product(h_ps[t][:, :HALF], W3, t, z_w[:, :HALF], z_s[:, :HALF])
            nc.scalar.copy(h_sb[t][:, :HALF], h_ps[t][:, :HALF])
        for t in SPLIT_TILES:
            gain(t, Z_SPLIT, S)
        interleave(nc.vector.tensor_copy, z_grp, z_rows, Z_SPLIT, S)
        quantize(z_w, z_s, z_grp, HALF, S)
        for t in range(PACK):
            product(h_ps[t][:, HALF:], W3, t, z_w[:, HALF:], z_s[:, HALF:])

        def spill_upper_h(t):
            (nc.vector.tensor_copy if t in (0, 1) else nc.scalar.copy)(h_sb[t][:, HALF:S], h_ps[t][:, HALF:])

        spill_upper_h(0)

        pa = sb("pa", [P, PACK, S], F32)
        pb = sb("pb", [P, PACK, S], F32)
        lo = sb("lo", [P, PACK, S], F32)
        hi = sb("hi", [P, PACK, S], F32)
        mid = sb("mid", [P, PACK, S], F32)
        res = sb("res", [P, PACK, S], F32)
        o_grp = sb("o_grp", [P, S, PACK], BF16)
        o_w = sb("o_w", [P, S], U32)
        o_s = sb("o_s", [P, S], U8)
        out_rows = out_0.rearrange("(p t) j -> p t j", t=PACK)
        out_words = out_1[0].rearrange("p n t -> p (n t)").bitcast(I32)

        def finish(t, a, b):
            nc.vector.tensor_tensor(res[:, t, a:b], lo[:, t, a:b], mid[:, t, a:b], ALU.max)
            nc.sync.dma_start(out_rows[:, t, a:b], res[:, t, a:b])

        steps = [(t, 0, S) for t in range(LAST)] + [(LAST, 0, HALF), (LAST, HALF, S)]
        for n, (t, a, b) in enumerate(steps):
            (fetch_vector if n == 0 else fetch_scalar)(pa[:, t, a:b], h_sb[t], n4_t, a, b)
            fetch_scalar(pb[:, t, a:b], h_sb[t], n5_t, a, b)
            if t < LAST:
                spill_upper_h(t + 1)
            nc.vector.tensor_tensor(hi[:, t, a:b], pa[:, t, a:b], h_ps[t][:, a:b], ALU.max)
            if n > 0:
                finish(*steps[n - 1])
            nc.vector.tensor_tensor(lo[:, t, a:b], pa[:, t, a:b], h_ps[t][:, a:b], ALU.min)
            nc.vector.tensor_tensor(mid[:, t, a:b], hi[:, t, a:b], pb[:, t, a:b], ALU.min)

        interleave(nc.scalar.copy, o_grp, res, 0, HALF)
        finish(*steps[-1])
        interleave(nc.vector.tensor_copy, o_grp, res, HALF, S)
        quantize(o_w, o_s, o_grp, 0, HALF)
        nc.sync.dma_start(out_words[:, :HALF], o_w[:, :HALF].bitcast(I32))
        quantize(o_w, o_s, o_grp, HALF, S)
        nc.scalar.dma_start(out_words[:, HALF:], o_w[:, HALF:].bitcast(I32))
        for q in range(PACK):
            queue = nc.scalar if q % 2 else nc.sync
            queue.dma_start(
                out_2[0, PACK * q : PACK * (q + 1), :].bitcast(I32),
                o_s[QUAD * q : QUAD * q + PACK, :].bitcast(I32),
            )
